import numpy as np
import ml_dtypes


def mxq(x, axis, fmt="e4m3"):
    dtype, down = {"e4m3": (ml_dtypes.float8_e4m3fn, 7), "e5m2": (ml_dtypes.float8_e5m2, 14)}[fmt]
    v = np.moveaxis(np.asarray(x, np.float32).astype(ml_dtypes.bfloat16).astype(np.float64), axis, -1)
    blocks = v.reshape(v.shape[:-1] + (-1, 32))
    amax = np.abs(blocks).max(-1, keepdims=True)
    byte = np.maximum(np.where(amax > 0, np.frexp(amax)[1] - 1 + 127, 0) - down, 1)
    scale = np.exp2(byte - 127.0)
    codes = (blocks / scale).astype(np.float32).astype(dtype).astype(np.float64)
    return np.moveaxis((codes * scale).reshape(v.shape), -1, axis)


WIDE = False


def mx_kscale(k):
    if not WIDE:
        return np.ones(k)
    levels = np.array([10, -10, 5, -5, 0])
    if k % 512:
        return np.exp2(np.random.permutation(np.resize(levels, k // 32))).repeat(32)
    a = np.empty((k // 512, 16))
    for p in range(k // 512):
        a[p, :8] = np.random.permutation(np.resize(levels, 8))
        for g in range(8):
            far = levels[np.abs(levels - a[p, g]) >= 10]
            a[p, g + 8] = far[np.random.randint(len(far))]
    return np.exp2(a.ravel()).repeat(32)


def f64(x):
    return np.asarray(x).astype(np.float64)


def striped(idx):
    return np.tile(idx.reshape(-1, 16).T, (8, 1)).astype(np.uint16)


def unstriped(offs):
    return offs[:16].T.reshape(-1).astype(np.int64)


E2M1 = np.array([0.0, 0.5, 1.0, 1.5, 2.0, 3.0, 4.0, 6.0, -0.0, -0.5, -1.0, -1.5, -2.0, -3.0, -4.0, -6.0])


def pack_weight(w, fmt):
    k, n = w.shape
    w = f64(np.asarray(w, np.float32).astype(ml_dtypes.bfloat16)).reshape(k // 32, 32, n)
    amax = np.abs(w).max(1)
    if fmt == "e4m3":
        byte = np.frexp(amax)[1] - 1 + 127 - 7
    else:
        mant, ex = np.frexp(amax / 6.0)
        byte = np.where(mant > 0.5, ex, ex - 1) + 127
    byte = np.clip(np.where(amax > 0, byte, 1), 1, 254)
    scaled = (w * np.exp2(127.0 - byte)[:, None, :]).reshape(k, n).astype(np.float32)
    by_word = np.ascontiguousarray(scaled.reshape(k // 512, 128, 4, n).transpose(0, 1, 3, 2))
    if fmt == "e4m3":
        words = by_word.astype(ml_dtypes.float8_e4m3fn).view(np.uint8)
    else:
        c = by_word.astype(ml_dtypes.float4_e2m1fn).view(np.uint8) & 0xF
        words = (c[..., 0::2] | (c[..., 1::2] << 4)).reshape(k // 512, 128, 2 * n)
    return np.ascontiguousarray(words), np.ascontiguousarray(byte.astype(np.uint8).reshape(k // 512, 16, n))


def unpack_weight(words, scales, fmt):
    g, _, n = scales.shape
    words = np.ascontiguousarray(words).reshape(g, 128, n, -1)
    if fmt == "e4m3":
        vals = words.view(ml_dtypes.float8_e4m3fn).astype(np.float64)
    else:
        nib = np.empty((g, 128, n, 4), np.uint8)
        nib[..., 0::2] = words & 0xF
        nib[..., 1::2] = words >> 4
        vals = E2M1[nib]
    vals = vals * np.repeat(np.exp2(scales.astype(np.float64) - 127.0), 8, axis=1)[..., None]
    return vals.transpose(0, 1, 3, 2).reshape(g * 512, n)


def gelu(v):
    return 0.5 * v * (1.0 + np.tanh(np.sqrt(2.0 / np.pi) * (v + 0.044715 * v**3)))


K, H, T, S, T3, S2, P = 1536, 512, 4096, 1024, 2048, 512, 512

def setup_inputs():
    n = np.random.standard_normal
    s = mx_kscale(K)[:, None]
    u = mx_kscale(H)[:, None]
    d = {}
    d["tab_words"], d["tab_scales"] = pack_weight(n((K, T)) * s, "e4m3")
    d["tab2_words"], d["tab2_scales"] = pack_weight(n((H, T3)) / H ** 0.5 / u, "e4m3")
    d["w1"] = (n((K, H)) / K ** 0.5 / s * u.T).astype(np.float32)
    d["w4_words"], d["w4_scales"] = pack_weight(n((K, H)) / K ** 0.5 / s * u.T, "e2m1")
    d["w8_words"], d["w8_scales"] = pack_weight(n((K, H)) / K ** 0.5 / s * u.T, "e4m3")
    d["gain"] = (2.0 * np.exp(0.5 * n(S2))).astype(np.float32)
    d["offs"] = striped(np.random.permutation(T)[:S])
    d["offs2"] = striped(np.random.permutation(T3)[:S2])
    d["pos1"] = striped(np.random.permutation(S)[:P])
    d["pos2"] = striped(np.random.permutation(S)[:P])
    return d

def reference(tab_words, tab_scales, tab2_words, tab2_scales, w1, w4_words, w4_scales,
              w8_words, w8_scales, gain, offs, offs2, pos1, pos2):
    v = unpack_weight(tab_words, tab_scales, "e4m3")[:, unstriped(offs)]
    v2 = unpack_weight(tab2_words, tab2_scales, "e4m3")[:, unstriped(offs2)]
    h1 = mxq(f64(w1), 0, "e4m3").T @ v
    h2 = unpack_weight(w4_words, w4_scales, "e2m1").T @ v
    h3 = unpack_weight(w8_words, w8_scales, "e4m3").T @ v
    h = np.maximum(np.maximum(h1, h2), h3)
    e = v2.T @ mxq(h, 0, "e4m3")
    pair = e[:, unstriped(pos1)] * e[:, unstriped(pos2)]
    return np.log(1.0 + f64(gain)[:, None] * np.abs(pair))

@@ -1,0 +1,247 @@
+from contextlib import ExitStack
+
+import concourse.mybir as mybir
+
+K, H, T, S, T3, S2, NP = 1536, 512, 4096, 1024, 2048, 512, 512
+FLOPS = 2 * (3 * K * H * S + H * S2 * S)
+
+F32 = mybir.dt.float32
+BF16 = mybir.dt.bfloat16
+I32 = mybir.dt.int32
+U32 = mybir.dt.uint32
+U16 = mybir.dt.uint16
+U8 = mybir.dt.uint8
+FP8X4 = mybir.dt.float8_e4m3fn_x4
+FP4X4 = mybir.dt.float4_e2m1fn_x4
+ACT = mybir.ActivationFunctionType
+ALU = mybir.AluOpType
+
+P = 128
+PASSES = K // 512
+HALF = S // 2
+JT = S // P
+
+
+def tile_list_accelerant_pair_scores_kernel(
+    tc, tab_words, tab_scales, tab2_words, tab2_scales, w1, w4_words, w4_scales,
+    w8_words, w8_scales, gain, offs, offs2, pos1, pos2, out,
+):
+    nc = tc.nc
+    with ExitStack() as ctx:
+        keep = ctx.enter_context(tc.tile_pool(name="keep", bufs=1))
+        psum = ctx.enter_context(tc.psum_pool(name="psum", bufs=1))
+
+        def sb(name, shape, dtype, tag=None):
+            return keep.tile(shape, dtype, name=name, tag=tag or name, align_bytes=64)
+
+        idx = keep.tile([P, S // 16], U16, name="idx")
+        idx2 = keep.tile([P, S2 // 16], U16, name="idx2")
+        p1 = keep.tile([P, NP // 16], U16, name="p1")
+        p2 = keep.tile([P, NP // 16], U16, name="p2")
+
+        table = [sb("table%d" % a, [P, T], U32) for a in range(PASSES)]
+        table_sc = sb("table_sc", [P, T], U8)
+        table2_sc = sb("table2_sc", [P, T3], U8)
+        v = [[None, None] for a in range(PASSES)]
+        v_sc = sb("v_sc", [P, S], U8)
+        v_sc_low = [v_sc] + [sb("v_sc_low%d" % a, [P, S], U8) for a in range(1, PASSES)]
+
+        w8_raw = sb("w8_raw", [P, PASSES, H], U32)
+        w8_sc_raw = sb("w8_sc_raw", [P, H], U8)
+        w4_raw = sb("w4_raw", [P, PASSES, H], U16)
+        w4_sc_raw = sb("w4_sc_raw", [P, PASSES, H], U8)
+        w8 = sb("w8", [P, PASSES, H], U32)
+        w8_sc = sb("w8_sc", [P, H], U8)
+        w4 = sb("w4", [P, PASSES, H], U16)
+        w4_sc = sb("w4_sc", [P, PASSES, H], U8)
+        w1_bf = []
+        w1q = [sb("w1q%d" % a, [P, H], U32) for a in range(PASSES)]
+        w1q_sc = [sb("w1q_sc%d" % a, [P, H], U8) for a in range(PASSES)]
+
+        best = [sb("best%d" % h, [P, 4, HALF], F32) for h in range(2)]
+        h_bf = [sb("h_bf%d" % j, [P, 4 * P], BF16) for j in range(JT)]
+        hq = [sb("hq%d" % h, [P, HALF], U32) for h in range(2)]
+        hq_sc = [sb("hq_sc%d" % h, [P, HALF], U8) for h in range(2)]
+        score = [sb("score%d" % i, [P, S], F32) for i in range(4)]
+        first = [sb("first%d" % i, [P, NP], F32) for i in range(4)]
+        pair = [sb("pair%d" % i, [P, NP], F32) for i in range(4)]
+        res = [sb("res%d" % i, [P, NP], F32) for i in range(4)]
+        gains = sb("gains", [P, 4], F32)
+        warm = sb("warm", [P, 2], F32)
+        bank = [psum.tile([P, 512], F32, name="bank%d" % b) for b in range(8)]
+
+        for plane in (table_sc, w8_sc_raw, w4_sc_raw, table2_sc, v_sc_low[1], v_sc_low[2]):
+            nc.vector.memset(plane[:].bitcast(I32), 0)
+        nc.vector.memset(warm[:, 0:1], 1.0)
+        nc.scalar.activation(out=warm[:, 1:2], in_=warm[:, 0:1], func=ACT.Ln)
+
+        def words(ap):
+            return ap.rearrange("p t i -> p (t i)").bitcast(I32)
+
+        nc.sync.dma_start(idx[:], offs)
+        nc.sync.dma_start(table[0][:].bitcast(I32), words(tab_words[0]))
+        nc.sync.dma_start(idx2[:], offs2)
+        nc.sync.dma_start(p1[:], pos1)
+        nc.sync.dma_start(p2[:], pos2)
+        for q in range(4):
+            nc.gpsimd.dma_start(table_sc[32 * q : 32 * q + 12, :].bitcast(I32), tab_scales[:, 4 * q : 4 * q + 4, :].bitcast(I32))
+        for q in range(4):
+            nc.scalar.dma_start(w8_sc_raw[32 * q : 32 * q + 12, :].bitcast(I32), w8_scales[:, 4 * q : 4 * q + 4, :].bitcast(I32))
+        nc.sync.dma_start(w8_raw[:].bitcast(I32), w8_words.rearrange("a p c i -> p a (c i)").bitcast(I32))
+        nc.sync.dma_start(table[1][:].bitcast(I32), words(tab_words[1]))
+        for q in range(4):
+            nc.scalar.dma_start(
+                w4_sc_raw[32 * q : 32 * q + 4, :, :].bitcast(I32),
+                w4_scales[:, 4 * q : 4 * q + 4, :].rearrange("a r c -> r a c").bitcast(I32),
+            )
+        nc.sync.dma_start(w4_raw[:].bitcast(I32), w4_words.rearrange("a p c -> p a c").bitcast(I32))
+        nc.sync.dma_start(table[2][:].bitcast(I32), words(tab_words[2]))
+        for q in range(4):
+            nc.gpsimd.dma_start(table2_sc[32 * q : 32 * q + 4, :].bitcast(I32), tab2_scales[0, 4 * q : 4 * q + 4, :].bitcast(I32))
+        with nc.allow_non_contiguous_dma(reason="one gain for each output row"):
+            nc.scalar.dma_start(gains[:], gain.rearrange("(i p) -> p i", p=P))
+
+        w1_raw = []
+
+        def load_w1(a, tag):
+            raw = sb("w1_raw%d" % a, [P, 4, H], F32, tag=tag)
+            nc.sync.dma_start(raw[:], w1[512 * a : 512 * (a + 1), :].rearrange("(p j) c -> p j c", j=4))
+            w1_raw.append(raw)
+
+        def gather_v(a, h, tag=None):
+            v[a][h] = sb("v%d_%d" % (a, h), [P, HALF], U32, tag=tag)
+            nc.vector.tensor_copy(v[a][h][:], table[a][:].indirect(idx[:, 32 * h : 32 * (h + 1)]))
+
+        def deal(dst, src):
+            nc.vector.tensor_copy(dst.rearrange("p a (t m) -> p a m t", t=4), src.rearrange("p a (m t) -> p a m t", t=4))
+
+        def cast_w1(on_vector, a, tag):
+            w1_bf.append(sb("w1_bf%d" % a, [P, 4 * H], BF16, tag=tag))
+            dst = w1_bf[a][:].rearrange("p (t m j) -> p m j t", t=4, j=4)
+            src = w1_raw[a][:].rearrange("p j (m t) -> p m j t", t=4)
+            if on_vector:
+                nc.vector.tensor_copy(dst, src)
+            else:
+                nc.scalar.copy(dst, src)
+
+        def quantize_w1(a):
+            nc.vector.quantize_mx(out=w1q[a][:].bitcast(FP8X4), scales=w1q_sc[a][:], in_=w1_bf[a][:])
+
+        def cols(t):
+            return slice(P * t, P * (t + 1))
+
+        def half(h):
+            return slice(HALF * h, HALF * (h + 1))
+
+        def mm_w8(h, t, a, start, stop):
+            nc.tensor.matmul_mx(
+                out=bank[4 * h + t][:], lhsT=w8[:, a, cols(t)].bitcast(FP8X4), lhsT_scale=w8_sc[4 * a : P, cols(t)],
+                rhs=v[a][h][:].bitcast(FP8X4), rhs_scale=v_sc[4 * a : P, half(h)], start=start, stop=stop,
+            )
+
+        def mm_w4(h, t, a):
+            nc.tensor.matmul_mx(
+                out=bank[4 * h + t][:], lhsT=w4[:, a, cols(t)].bitcast(FP4X4), lhsT_scale=w4_sc[:, a, cols(t)],
+                rhs=v[a][h][:].bitcast(FP8X4), rhs_scale=v_sc_low[a][:, half(h)], start=(a == 0), stop=(a == PASSES - 1),
+            )
+
+        def mm_w1(j, a):
+            for t in range(4):
+                nc.tensor.matmul_mx(
+                    out=bank[j][:, cols(t)], lhsT=w1q[a][:, cols(t)].bitcast(FP8X4), lhsT_scale=w1q_sc[a][:, cols(t)],
+                    rhs=v[a][j // 4][:, cols(j % 4)].bitcast(FP8X4), rhs_scale=v_sc[4 * a : P, cols(j)],
+                    start=(a == 0 and t == 0), stop=(a == PASSES - 1 and t == 3),
+                )
+
+        def last_max(j):
+            nc.vector.tensor_tensor(
+                h_bf[j][:].rearrange("p (c i t) -> p c t i", i=4, t=4),
+                bank[j][:].rearrange("p (t c i) -> p c t i", t=4, i=4),
+                best[j // 4][:, :, cols(j % 4)].rearrange("p t (c i) -> p c t i", i=4),
+                ALU.max,
+            )
+
+        def quantize_h(j):
+            nc.vector.quantize_mx(out=hq[j // 4][:, cols(j % 4)].bitcast(FP8X4), scales=hq_sc[j // 4][:, cols(j % 4)], in_=h_bf[j][:])
+
+        def scores(i, b, lo, hi):
+            h, n = lo // HALF, hi - lo
+            part = slice(lo - HALF * h, hi - HALF * h)
+            nc.tensor.matmul_mx(
+                out=bank[b][:, 0:n], lhsT=v2[:, cols(i)].bitcast(FP8X4), lhsT_scale=v2_sc[:, cols(i)],
+                rhs=hq[h][:, part].bitcast(FP8X4), rhs_scale=hq_sc[h][:, part], start=True, stop=True,
+            )
+            nc.scalar.activation(out=score[i][:, lo:hi], in_=bank[b][:, 0:n], func=ACT.Abs)
+
+        nc.vector.tensor_copy(v_sc[:], table_sc[:].indirect(idx[:]))
+        for a in range(1, PASSES):
+            nc.scalar.dma_start(v_sc_low[a][0:100, :].bitcast(I32), v_sc[4 * a : 4 * a + 100, :].bitcast(I32))
+        gather_v(0, 0, tag="table_sc")
+        gather_v(0, 1)
+        load_w1(0, "table0")
+        deal(w8[:], w8_raw[:])
+        load_w1(1, "w8_raw")
+        deal(w8_sc[:].unsqueeze(1), w8_sc_raw[:].unsqueeze(1))
+        gather_v(1, 0)
+        gather_v(1, 1)
+        load_w1(2, "table1")
+        for h in range(2):
+            for a in (1, 0):
+                for t in range(4):
+                    mm_w8(h, t, a, start=(a == 1), stop=False)
+        deal(w4[:], w4_raw[:])
+        deal(w4_sc[:], w4_sc_raw[:])
+        table2 = sb("table2", [P, T3], U32, tag="w4_raw")
+        nc.sync.dma_start(table2[:].bitcast(I32), words(tab2_words[0]))
+        for h in range(2):
+            gather_v(2, h)
+            for t in range(4):
+                mm_w8(h, t, 2, start=False, stop=True)
+                nc.scalar.copy(best[h][:, t, :], bank[4 * h + t][:])
+        cast_w1(True, 0, None)
+        quantize_w1(0)
+        cast_w1(False, 1, "w8")
+        cast_w1(False, 2, "w8_sc")
+        for h in range(2):
+            for t in range(4):
+                for a in range(PASSES):
+                    mm_w4(h, t, a)
+                nc.vector.tensor_tensor(best[h][:, t, :], bank[4 * h + t][:], best[h][:, t, :], ALU.max)
+            if h == 0:
+                quantize_w1(1)
+        quantize_w1(2)
+        v2 = sb("v2", [P, S2], U32, tag="w8_raw")
+        nc.vector.tensor_copy(v2[:], table2[:].indirect(idx2[:]))
+        v2_sc = sb("v2_sc", [P, S2], U8, tag="table1")
+        nc.vector.tensor_copy(v2_sc[:], table2_sc[:].indirect(idx2[:]))
+        for j in range(JT):
+            for a in range(PASSES):
+                mm_w1(j, a)
+            last_max(j)
+            if j > 0:
+                quantize_h(j - 1)
+            if j == 5:
+                scores(0, 0, 0, 512)
+            if j == 7:
+                scores(0, 1, 512, 768)
+                scores(0, 2, 768, 896)
+        quantize_h(JT - 1)
+        scores(0, 3, 896, 1024)
+        for i in range(1, 4):
+            for h in range(2):
+                scores(i, (2 + 2 * i + h) % 8, HALF * h, HALF * (h + 1))
+
+        def pick_first(i, lo, hi):
+            nc.vector.tensor_copy(first[i][:, lo:hi], score[i][:].indirect(p1[:, lo // 16 : hi // 16]))
+
+        def finish(i, lo, hi):
+            nc.vector.tensor_tensor(pair[i][:, lo:hi], score[i][:].indirect(p2[:, lo // 16 : hi // 16]), first[i][:, lo:hi], ALU.mult)
+            nc.scalar.activation(out=res[i][:, lo:hi], in_=pair[i][:, lo:hi], func=ACT.Ln, bias=1.0, scale=gains[:, i : i + 1])
+            nc.sync.dma_start(out[cols(i), lo:hi], res[i][:, lo:hi])
+
+        pick_first(0, 0, NP)
+        for i in range(3):
+            pick_first(i + 1, 0, NP)
+            finish(i, 0, NP)
+        finish(3, 0, NP // 2)
+        finish(3, NP // 2, NP)

@@ -20,6 +20,13 @@ P = 128
 PASSES = K // 512
 HALF = S // 2
 JT = S // P
+KB = 1024
+TABLE_AT = (0, 16 * KB, 34 * KB)
+W4_SC_RAW_AT = 32 * KB
+TABLE_SC_AT = 50 * KB
+W8_SC_RAW_AT = 54 * KB
+W8_RAW_AT = 55 * KB
+W8_AT = 66 * KB
 
 
 def tile_list_accelerant_pair_scores_kernel(
@@ -29,32 +36,33 @@ def tile_list_accelerant_pair_scores_kernel(
     nc = tc.nc
     with ExitStack() as ctx:
         keep = ctx.enter_context(tc.tile_pool(name="keep", bufs=1))
+        turns = ctx.enter_context(tc.tile_pool(name="turns", bufs=1))
         psum = ctx.enter_context(tc.psum_pool(name="psum", bufs=1))
 
-        def sb(name, shape, dtype, tag=None):
-            return keep.tile(shape, dtype, name=name, tag=tag or name, align_bytes=64)
+        def sb(name, shape, dtype, at=None):
+            if at is None:
+                return keep.tile(shape, dtype, name=name, align_bytes=64)
+            return turns.tile(shape, dtype, name=name, offset=at, align_bytes=64)
 
         idx = keep.tile([P, S // 16], U16, name="idx")
         idx2 = keep.tile([P, S2 // 16], U16, name="idx2")
         p1 = keep.tile([P, NP // 16], U16, name="p1")
         p2 = keep.tile([P, NP // 16], U16, name="p2")
 
-        table = [sb("table%d" % a, [P, T], U32) for a in range(PASSES)]
-        table_sc = sb("table_sc", [P, T], U8)
+        table = [sb("table%d" % a, [P, T], U32, at=TABLE_AT[a]) for a in range(PASSES)]
+        table_sc = sb("table_sc", [P, T], U8, at=TABLE_SC_AT)
         table2_sc = sb("table2_sc", [P, T3], U8)
         v = [[None, None] for a in range(PASSES)]
         v_sc = sb("v_sc", [P, S], U8)
         v_sc_low = [v_sc] + [sb("v_sc_low%d" % a, [P, S], U8) for a in range(1, PASSES)]
 
-        w8_raw = sb("w8_raw", [P, PASSES, H], U32)
-        w8_sc_raw = sb("w8_sc_raw", [P, H], U8)
+        w8_raw = sb("w8_raw", [P, PASSES, H], U32, at=W8_RAW_AT)
         w4_raw = sb("w4_raw", [P, PASSES, H], U16)
-        w4_sc_raw = sb("w4_sc_raw", [P, PASSES, H], U8)
-        w8 = sb("w8", [P, PASSES, H], U32)
+        w8_sc_raw = sb("w8_sc_raw", [P, H], U8, at=W8_SC_RAW_AT)
+        w4_sc_raw = sb("w4_sc_raw", [P, PASSES, H], U8, at=W4_SC_RAW_AT)
+        w8 = sb("w8", [P, PASSES, H], U32, at=W8_AT)
         w8_sc = sb("w8_sc", [P, H], U8)
-        w4 = sb("w4", [P, PASSES, H], U16)
         w4_sc = sb("w4_sc", [P, PASSES, H], U8)
-        w1_bf = []
         w1q = [sb("w1q%d" % a, [P, H], U32) for a in range(PASSES)]
         w1q_sc = [sb("w1q_sc%d" % a, [P, H], U8) for a in range(PASSES)]
 
@@ -66,11 +74,11 @@ def tile_list_accelerant_pair_scores_kernel(
         first = [sb("first%d" % i, [P, NP], F32) for i in range(4)]
         pair = [sb("pair%d" % i, [P, NP], F32) for i in range(4)]
         res = [sb("res%d" % i, [P, NP], F32) for i in range(4)]
-        gains = sb("gains", [P, 4], F32)
         warm = sb("warm", [P, 2], F32)
         bank = [psum.tile([P, 512], F32, name="bank%d" % b) for b in range(8)]
 
-        for plane in (table_sc, w8_sc_raw, w4_sc_raw, table2_sc, v_sc_low[1], v_sc_low[2]):
+        nc.gpsimd.memset(table_sc[:].bitcast(I32), 0)
+        for plane in (w4_sc_raw, w8_sc_raw, table2_sc, v_sc_low[1], v_sc_low[2]):
             nc.vector.memset(plane[:].bitcast(I32), 0)
         nc.vector.memset(warm[:, 0:1], 1.0)
         nc.scalar.activation(out=warm[:, 1:2], in_=warm[:, 0:1], func=ACT.Ln)
@@ -86,46 +94,44 @@ def tile_list_accelerant_pair_scores_kernel(
         for q in range(4):
             nc.gpsimd.dma_start(table_sc[32 * q : 32 * q + 12, :].bitcast(I32), tab_scales[:, 4 * q : 4 * q + 4, :].bitcast(I32))
         for q in range(4):
-            nc.scalar.dma_start(w8_sc_raw[32 * q : 32 * q + 12, :].bitcast(I32), w8_scales[:, 4 * q : 4 * q + 4, :].bitcast(I32))
-        nc.sync.dma_start(w8_raw[:].bitcast(I32), w8_words.rearrange("a p c i -> p a (c i)").bitcast(I32))
-        nc.sync.dma_start(table[1][:].bitcast(I32), words(tab_words[1]))
+            nc.gpsimd.dma_start(w8_sc_raw[32 * q : 32 * q + 12, :].bitcast(I32), w8_scales[:, 4 * q : 4 * q + 4, :].bitcast(I32))
         for q in range(4):
             nc.scalar.dma_start(
                 w4_sc_raw[32 * q : 32 * q + 4, :, :].bitcast(I32),
                 w4_scales[:, 4 * q : 4 * q + 4, :].rearrange("a r c -> r a c").bitcast(I32),
             )
+        nc.sync.dma_start(w8_raw[:].bitcast(I32), w8_words.rearrange("a p c i -> p a (c i)").bitcast(I32))
+        nc.sync.dma_start(table[1][:].bitcast(I32), words(tab_words[1]))
         nc.sync.dma_start(w4_raw[:].bitcast(I32), w4_words.rearrange("a p c -> p a c").bitcast(I32))
         nc.sync.dma_start(table[2][:].bitcast(I32), words(tab_words[2]))
         for q in range(4):
             nc.gpsimd.dma_start(table2_sc[32 * q : 32 * q + 4, :].bitcast(I32), tab2_scales[0, 4 * q : 4 * q + 4, :].bitcast(I32))
-        with nc.allow_non_contiguous_dma(reason="one gain for each output row"):
-            nc.scalar.dma_start(gains[:], gain.rearrange("(i p) -> p i", p=P))
 
         w1_raw = []
 
-        def load_w1(a, tag):
-            raw = sb("w1_raw%d" % a, [P, 4, H], F32, tag=tag)
+        def load_w1(a, at):
+            raw = sb("w1_raw%d" % a, [P, 4, H], F32, at=at)
             nc.sync.dma_start(raw[:], w1[512 * a : 512 * (a + 1), :].rearrange("(p j) c -> p j c", j=4))
             w1_raw.append(raw)
 
-        def gather_v(a, h, tag=None):
-            v[a][h] = sb("v%d_%d" % (a, h), [P, HALF], U32, tag=tag)
+        def gather_v(a, h, at=None):
+            v[a][h] = sb("v%d_%d" % (a, h), [P, HALF], U32, at=at)
             nc.vector.tensor_copy(v[a][h][:], table[a][:].indirect(idx[:, 32 * h : 32 * (h + 1)]))
 
         def deal(dst, src):
             nc.vector.tensor_copy(dst.rearrange("p a (t m) -> p a m t", t=4), src.rearrange("p a (m t) -> p a m t", t=4))
 
-        def cast_w1(on_vector, a, tag):
-            w1_bf.append(sb("w1_bf%d" % a, [P, 4 * H], BF16, tag=tag))
-            dst = w1_bf[a][:].rearrange("p (t m j) -> p m j t", t=4, j=4)
-            src = w1_raw[a][:].rearrange("p j (m t) -> p m j t", t=4)
-            if on_vector:
-                nc.vector.tensor_copy(dst, src)
-            else:
-                nc.scalar.copy(dst, src)
+        def cast_w1(copy, a, t0, t1, at):
+            rounded = sb("w1_bf%d_%d" % (a, t0), [P, (t1 - t0) * H], BF16, at=at)
+            copy(
+                rounded[:].rearrange("p (t m j) -> p m j t", m=P, j=4),
+                w1_raw[a][:].rearrange("p j (m t) -> p m j t", t=4)[:, :, :, t0:t1],
+            )
+            return rounded
 
-        def quantize_w1(a):
-            nc.vector.quantize_mx(out=w1q[a][:].bitcast(FP8X4), scales=w1q_sc[a][:], in_=w1_bf[a][:])
+        def quantize_w1(rounded, a, t0, t1):
+            part = slice(P * t0, P * t1)
+            nc.vector.quantize_mx(out=w1q[a][:, part].bitcast(FP8X4), scales=w1q_sc[a][:, part], in_=rounded[:])
 
         def cols(t):
             return slice(P * t, P * (t + 1))
@@ -173,47 +179,49 @@ def tile_list_accelerant_pair_scores_kernel(
             )
             nc.scalar.activation(out=score[i][:, lo:hi], in_=bank[b][:, 0:n], func=ACT.Abs)
 
+        gather_v(0, 0)
+        gather_v(0, 1)
+        table2 = sb("table2", [P, T3], U32, at=TABLE_AT[0])
+        nc.sync.dma_start(table2[:].bitcast(I32), words(tab2_words[0]))
+        load_w1(0, TABLE_AT[0] + 8 * KB)
+        deal(w8[:], w8_raw[:])
+        load_w1(1, W8_RAW_AT)
         nc.vector.tensor_copy(v_sc[:], table_sc[:].indirect(idx[:]))
         for a in range(1, PASSES):
             nc.scalar.dma_start(v_sc_low[a][0:100, :].bitcast(I32), v_sc[4 * a : 4 * a + 100, :].bitcast(I32))
-        gather_v(0, 0, tag="table_sc")
-        gather_v(0, 1)
-        load_w1(0, "table0")
-        deal(w8[:], w8_raw[:])
-        load_w1(1, "w8_raw")
         deal(w8_sc[:].unsqueeze(1), w8_sc_raw[:].unsqueeze(1))
-        gather_v(1, 0)
-        gather_v(1, 1)
-        load_w1(2, "table1")
+        deal(w4_sc[:], w4_sc_raw[:])
+        gains = sb("gains", [P, 4], F32, at=W4_SC_RAW_AT + KB + 256)
+        with nc.allow_non_contiguous_dma(reason="one gain for each output row"):
+            nc.sync.dma_start(gains[:], gain.rearrange("(i p) -> p i", p=P))
+        gather_v(1, 0, at=TABLE_SC_AT + 2 * KB + 256)
+        gather_v(1, 1, at=TABLE_SC_AT)
+        load_w1(2, TABLE_AT[1])
         for h in range(2):
             for a in (1, 0):
                 for t in range(4):
                     mm_w8(h, t, a, start=(a == 1), stop=False)
+        w4 = sb("w4", [P, PASSES, H], U16, at=TABLE_AT[1] + 10 * KB)
         deal(w4[:], w4_raw[:])
-        deal(w4_sc[:], w4_sc_raw[:])
-        table2 = sb("table2", [P, T3], U32, tag="w4_raw")
-        nc.sync.dma_start(table2[:].bitcast(I32), words(tab2_words[0]))
         for h in range(2):
-            gather_v(2, h)
+            gather_v(2, h, at=TABLE_AT[1] + (15 * KB, 8 * KB)[h])
             for t in range(4):
                 mm_w8(h, t, 2, start=False, stop=True)
                 nc.scalar.copy(best[h][:, t, :], bank[4 * h + t][:])
-        cast_w1(True, 0, None)
-        quantize_w1(0)
-        cast_w1(False, 1, "w8")
-        cast_w1(False, 2, "w8_sc")
+        v2 = sb("v2", [P, S2], U32, at=TABLE_AT[2])
+        nc.vector.tensor_copy(v2[:], table2[:].indirect(idx2[:]))
+        v2_sc = sb("v2_sc", [P, S2], U8, at=TABLE_AT[2] + 2 * KB)
+        nc.vector.tensor_copy(v2_sc[:], table2_sc[:].indirect(idx2[:]))
+        rounded = [cast_w1(nc.scalar.copy, a, 0, (4, 4, 2)[a], W8_AT + (4 * a - 3) * KB) for a in range(PASSES)]
         for h in range(2):
             for t in range(4):
                 for a in range(PASSES):
                     mm_w4(h, t, a)
                 nc.vector.tensor_tensor(best[h][:, t, :], bank[4 * h + t][:], best[h][:, t, :], ALU.max)
-            if h == 0:
-                quantize_w1(1)
-        quantize_w1(2)
-        v2 = sb("v2", [P, S2], U32, tag="w8_raw")
-        nc.vector.tensor_copy(v2[:], table2[:].indirect(idx2[:]))
-        v2_sc = sb("v2_sc", [P, S2], U8, tag="table1")
-        nc.vector.tensor_copy(v2_sc[:], table2_sc[:].indirect(idx2[:]))
+            quantize_w1(rounded[h], h, 0, 4)
+        rest = cast_w1(nc.vector.tensor_copy, 2, 2, 4, TABLE_AT[1] + 10 * KB)
+        quantize_w1(rounded[2], 2, 0, 2)
+        quantize_w1(rest, 2, 2, 4)
         for j in range(JT):
             for a in range(PASSES):
                 mm_w1(j, a)

from contextlib import ExitStack

import concourse.mybir as mybir

K, H, T, S, T3, S2, NP = 1536, 512, 4096, 1024, 2048, 512, 512
FLOPS = 2 * (3 * K * H * S + H * S2 * S)

F32 = mybir.dt.float32
BF16 = mybir.dt.bfloat16
I32 = mybir.dt.int32
U32 = mybir.dt.uint32
U16 = mybir.dt.uint16
U8 = mybir.dt.uint8
FP8X4 = mybir.dt.float8_e4m3fn_x4
FP4X4 = mybir.dt.float4_e2m1fn_x4
ACT = mybir.ActivationFunctionType
ALU = mybir.AluOpType

P = 128
PASSES = K // 512
HALF = S // 2
JT = S // P
KB = 1024
TABLE_AT = (0, 16 * KB, 34 * KB)
W4_SC_RAW_AT = 32 * KB
TABLE_SC_AT = 50 * KB
W8_SC_RAW_AT = 54 * KB
W8_RAW_AT = 55 * KB
W8_AT = 66 * KB


def tile_list_accelerant_pair_scores_kernel(
    tc, tab_words, tab_scales, tab2_words, tab2_scales, w1, w4_words, w4_scales,
    w8_words, w8_scales, gain, offs, offs2, pos1, pos2, out,
):
    nc = tc.nc
    with ExitStack() as ctx:
        keep = ctx.enter_context(tc.tile_pool(name="keep", bufs=1))
        turns = ctx.enter_context(tc.tile_pool(name="turns", bufs=1))
        psum = ctx.enter_context(tc.psum_pool(name="psum", bufs=1))

        def sb(name, shape, dtype, at=None):
            if at is None:
                return keep.tile(shape, dtype, name=name, align_bytes=64)
            return turns.tile(shape, dtype, name=name, offset=at, align_bytes=64)

        idx = keep.tile([P, S // 16], U16, name="idx")
        idx2 = keep.tile([P, S2 // 16], U16, name="idx2")
        p1 = keep.tile([P, NP // 16], U16, name="p1")
        p2 = keep.tile([P, NP // 16], U16, name="p2")

        table = [sb("table%d" % a, [P, T], U32, at=TABLE_AT[a]) for a in range(PASSES)]
        table_sc = sb("table_sc", [P, T], U8, at=TABLE_SC_AT)
        table2_sc = sb("table2_sc", [P, T3], U8)
        v = [[None, None] for a in range(PASSES)]
        v_sc = sb("v_sc", [P, S], U8)
        v_sc_low = [v_sc] + [sb("v_sc_low%d" % a, [P, S], U8) for a in range(1, PASSES)]

        w8_raw = sb("w8_raw", [P, PASSES, H], U32, at=W8_RAW_AT)
        w4_raw = sb("w4_raw", [P, PASSES, H], U16)
        w8_sc_raw = sb("w8_sc_raw", [P, H], U8, at=W8_SC_RAW_AT)
        w4_sc_raw = sb("w4_sc_raw", [P, PASSES, H], U8, at=W4_SC_RAW_AT)
        w8 = sb("w8", [P, PASSES, H], U32, at=W8_AT)
        w8_sc = sb("w8_sc", [P, H], U8)
        w4_sc = sb("w4_sc", [P, PASSES, H], U8)
        w1q = [sb("w1q%d" % a, [P, H], U32) for a in range(PASSES)]
        w1q_sc = [sb("w1q_sc%d" % a, [P, H], U8) for a in range(PASSES)]

        best = [sb("best%d" % h, [P, 4, HALF], F32) for h in range(2)]
        h_bf = [sb("h_bf%d" % j, [P, 4 * P], BF16) for j in range(JT)]
        hq = [sb("hq%d" % h, [P, HALF], U32) for h in range(2)]
        hq_sc = [sb("hq_sc%d" % h, [P, HALF], U8) for h in range(2)]
        score = [sb("score%d" % i, [P, S], F32) for i in range(4)]
        first = [sb("first%d" % i, [P, NP], F32) for i in range(4)]
        pair = [sb("pair%d" % i, [P, NP], F32) for i in range(4)]
        res = [sb("res%d" % i, [P, NP], F32) for i in range(4)]
        warm = sb("warm", [P, 2], F32)
        bank = [psum.tile([P, 512], F32, name="bank%d" % b) for b in range(8)]

        nc.gpsimd.memset(table_sc[:].bitcast(I32), 0)
        for plane in (w4_sc_raw, w8_sc_raw, table2_sc, v_sc_low[1], v_sc_low[2]):
            nc.vector.memset(plane[:].bitcast(I32), 0)
        nc.vector.memset(warm[:, 0:1], 1.0)
        nc.scalar.activation(out=warm[:, 1:2], in_=warm[:, 0:1], func=ACT.Ln)

        def words(ap):
            return ap.rearrange("p t i -> p (t i)").bitcast(I32)

        nc.sync.dma_start(idx[:], offs)
        nc.sync.dma_start(table[0][:].bitcast(I32), words(tab_words[0]))
        nc.sync.dma_start(idx2[:], offs2)
        nc.sync.dma_start(p1[:], pos1)
        nc.sync.dma_start(p2[:], pos2)
        for q in range(4):
            nc.gpsimd.dma_start(table_sc[32 * q : 32 * q + 12, :].bitcast(I32), tab_scales[:, 4 * q : 4 * q + 4, :].bitcast(I32))
        for q in range(4):
            nc.gpsimd.dma_start(w8_sc_raw[32 * q : 32 * q + 12, :].bitcast(I32), w8_scales[:, 4 * q : 4 * q + 4, :].bitcast(I32))
        for q in range(4):
            nc.scalar.dma_start(
                w4_sc_raw[32 * q : 32 * q + 4, :, :].bitcast(I32),
                w4_scales[:, 4 * q : 4 * q + 4, :].rearrange("a r c -> r a c").bitcast(I32),
            )
        nc.sync.dma_start(w8_raw[:].bitcast(I32), w8_words.rearrange("a p c i -> p a (c i)").bitcast(I32))
        nc.sync.dma_start(table[1][:].bitcast(I32), words(tab_words[1]))
        nc.sync.dma_start(w4_raw[:].bitcast(I32), w4_words.rearrange("a p c -> p a c").bitcast(I32))
        nc.sync.dma_start(table[2][:].bitcast(I32), words(tab_words[2]))
        for q in range(4):
            nc.gpsimd.dma_start(table2_sc[32 * q : 32 * q + 4, :].bitcast(I32), tab2_scales[0, 4 * q : 4 * q + 4, :].bitcast(I32))

        w1_raw = []

        def load_w1(a, at):
            raw = sb("w1_raw%d" % a, [P, 4, H], F32, at=at)
            nc.sync.dma_start(raw[:], w1[512 * a : 512 * (a + 1), :].rearrange("(p j) c -> p j c", j=4))
            w1_raw.append(raw)

        def gather_v(a, h, at=None):
            v[a][h] = sb("v%d_%d" % (a, h), [P, HALF], U32, at=at)
            nc.vector.tensor_copy(v[a][h][:], table[a][:].indirect(idx[:, 32 * h : 32 * (h + 1)]))

        def deal(dst, src):
            nc.vector.tensor_copy(dst.rearrange("p a (t m) -> p a m t", t=4), src.rearrange("p a (m t) -> p a m t", t=4))

        def cast_w1(copy, a, t0, t1, at):
            rounded = sb("w1_bf%d_%d" % (a, t0), [P, (t1 - t0) * H], BF16, at=at)
            copy(
                rounded[:].rearrange("p (t m j) -> p m j t", m=P, j=4),
                w1_raw[a][:].rearrange("p j (m t) -> p m j t", t=4)[:, :, :, t0:t1],
            )
            return rounded

        def quantize_w1(rounded, a, t0, t1):
            part = slice(P * t0, P * t1)
            nc.vector.quantize_mx(out=w1q[a][:, part].bitcast(FP8X4), scales=w1q_sc[a][:, part], in_=rounded[:])

        def cols(t):
            return slice(P * t, P * (t + 1))

        def half(h):
            return slice(HALF * h, HALF * (h + 1))

        def mm_w8(h, t, a, start, stop):
            nc.tensor.matmul_mx(
                out=bank[4 * h + t][:], lhsT=w8[:, a, cols(t)].bitcast(FP8X4), lhsT_scale=w8_sc[4 * a : P, cols(t)],
                rhs=v[a][h][:].bitcast(FP8X4), rhs_scale=v_sc[4 * a : P, half(h)], start=start, stop=stop,
            )

        def mm_w4(h, t, a):
            nc.tensor.matmul_mx(
                out=bank[4 * h + t][:], lhsT=w4[:, a, cols(t)].bitcast(FP4X4), lhsT_scale=w4_sc[:, a, cols(t)],
                rhs=v[a][h][:].bitcast(FP8X4), rhs_scale=v_sc_low[a][:, half(h)], start=(a == 0), stop=(a == PASSES - 1),
            )

        def mm_w1(j, a):
            for t in range(4):
                nc.tensor.matmul_mx(
                    out=bank[j][:, cols(t)], lhsT=w1q[a][:, cols(t)].bitcast(FP8X4), lhsT_scale=w1q_sc[a][:, cols(t)],
                    rhs=v[a][j // 4][:, cols(j % 4)].bitcast(FP8X4), rhs_scale=v_sc[4 * a : P, cols(j)],
                    start=(a == 0 and t == 0), stop=(a == PASSES - 1 and t == 3),
                )

        def last_max(j):
            nc.vector.tensor_tensor(
                h_bf[j][:].rearrange("p (c i t) -> p c t i", i=4, t=4),
                bank[j][:].rearrange("p (t c i) -> p c t i", t=4, i=4),
                best[j // 4][:, :, cols(j % 4)].rearrange("p t (c i) -> p c t i", i=4),
                ALU.max,
            )

        def quantize_h(j):
            nc.vector.quantize_mx(out=hq[j // 4][:, cols(j % 4)].bitcast(FP8X4), scales=hq_sc[j // 4][:, cols(j % 4)], in_=h_bf[j][:])

        def scores(i, b, lo, hi):
            h, n = lo // HALF, hi - lo
            part = slice(lo - HALF * h, hi - HALF * h)
            nc.tensor.matmul_mx(
                out=bank[b][:, 0:n], lhsT=v2[:, cols(i)].bitcast(FP8X4), lhsT_scale=v2_sc[:, cols(i)],
                rhs=hq[h][:, part].bitcast(FP8X4), rhs_scale=hq_sc[h][:, part], start=True, stop=True,
            )
            nc.scalar.activation(out=score[i][:, lo:hi], in_=bank[b][:, 0:n], func=ACT.Abs)

        gather_v(0, 0)
        gather_v(0, 1)
        table2 = sb("table2", [P, T3], U32, at=TABLE_AT[0])
        nc.sync.dma_start(table2[:].bitcast(I32), words(tab2_words[0]))
        load_w1(0, TABLE_AT[0] + 8 * KB)
        deal(w8[:], w8_raw[:])
        load_w1(1, W8_RAW_AT)
        nc.vector.tensor_copy(v_sc[:], table_sc[:].indirect(idx[:]))
        for a in range(1, PASSES):
            nc.scalar.dma_start(v_sc_low[a][0:100, :].bitcast(I32), v_sc[4 * a : 4 * a + 100, :].bitcast(I32))
        deal(w8_sc[:].unsqueeze(1), w8_sc_raw[:].unsqueeze(1))
        deal(w4_sc[:], w4_sc_raw[:])
        gains = sb("gains", [P, 4], F32, at=W4_SC_RAW_AT + KB + 256)
        with nc.allow_non_contiguous_dma(reason="one gain for each output row"):
            nc.sync.dma_start(gains[:], gain.rearrange("(i p) -> p i", p=P))
        gather_v(1, 0, at=TABLE_SC_AT + 2 * KB + 256)
        gather_v(1, 1, at=TABLE_SC_AT)
        load_w1(2, TABLE_AT[1])
        for h in range(2):
            for a in (1, 0):
                for t in range(4):
                    mm_w8(h, t, a, start=(a == 1), stop=False)
        w4 = sb("w4", [P, PASSES, H], U16, at=TABLE_AT[1] + 10 * KB)
        deal(w4[:], w4_raw[:])
        for h in range(2):
            gather_v(2, h, at=TABLE_AT[1] + (15 * KB, 8 * KB)[h])
            for t in range(4):
                mm_w8(h, t, 2, start=False, stop=True)
                nc.scalar.copy(best[h][:, t, :], bank[4 * h + t][:])
        v2 = sb("v2", [P, S2], U32, at=TABLE_AT[2])
        nc.vector.tensor_copy(v2[:], table2[:].indirect(idx2[:]))
        v2_sc = sb("v2_sc", [P, S2], U8, at=TABLE_AT[2] + 2 * KB)
        nc.vector.tensor_copy(v2_sc[:], table2_sc[:].indirect(idx2[:]))
        rounded = [cast_w1(nc.scalar.copy, a, 0, (4, 4, 2)[a], W8_AT + (4 * a - 3) * KB) for a in range(PASSES)]
        for h in range(2):
            for t in range(4):
                for a in range(PASSES):
                    mm_w4(h, t, a)
                nc.vector.tensor_tensor(best[h][:, t, :], bank[4 * h + t][:], best[h][:, t, :], ALU.max)
            quantize_w1(rounded[h], h, 0, 4)
        rest = cast_w1(nc.vector.tensor_copy, 2, 2, 4, TABLE_AT[1] + 10 * KB)
        quantize_w1(rounded[2], 2, 0, 2)
        quantize_w1(rest, 2, 2, 4)
        for j in range(JT):
            for a in range(PASSES):
                mm_w1(j, a)
            last_max(j)
            if j > 0:
                quantize_h(j - 1)
            if j == 5:
                scores(0, 0, 0, 512)
            if j == 7:
                scores(0, 1, 512, 768)
                scores(0, 2, 768, 896)
        quantize_h(JT - 1)
        scores(0, 3, 896, 1024)
        for i in range(1, 4):
            for h in range(2):
                scores(i, (2 + 2 * i + h) % 8, HALF * h, HALF * (h + 1))

        def pick_first(i, lo, hi):
            nc.vector.tensor_copy(first[i][:, lo:hi], score[i][:].indirect(p1[:, lo // 16 : hi // 16]))

        def finish(i, lo, hi):
            nc.vector.tensor_tensor(pair[i][:, lo:hi], score[i][:].indirect(p2[:, lo // 16 : hi // 16]), first[i][:, lo:hi], ALU.mult)
            nc.scalar.activation(out=res[i][:, lo:hi], in_=pair[i][:, lo:hi], func=ACT.Ln, bias=1.0, scale=gains[:, i : i + 1])
            nc.sync.dma_start(out[cols(i), lo:hi], res[i][:, lo:hi])

        pick_first(0, 0, NP)
        for i in range(3):
            pick_first(i + 1, 0, NP)
            finish(i, 0, NP)
        finish(3, 0, NP // 2)
        finish(3, NP // 2, NP)
